import numpy as np
import ml_dtypes


def mxq(x, axis, fmt="e4m3"):
    dtype, down = {"e4m3": (ml_dtypes.float8_e4m3fn, 7), "e5m2": (ml_dtypes.float8_e5m2, 14)}[fmt]
    v = np.moveaxis(np.asarray(x, np.float32).astype(ml_dtypes.bfloat16).astype(np.float64), axis, -1)
    blocks = v.reshape(v.shape[:-1] + (-1, 32))
    amax = np.abs(blocks).max(-1, keepdims=True)
    byte = np.maximum(np.where(amax > 0, np.frexp(amax)[1] - 1 + 127, 0) - down, 1)
    scale = np.exp2(byte - 127.0)
    codes = (blocks / scale).astype(np.float32).astype(dtype).astype(np.float64)
    return np.moveaxis((codes * scale).reshape(v.shape), -1, axis)


WIDE = False


def mx_kscale(k):
    if not WIDE:
        return np.ones(k)
    levels = np.array([10, -10, 5, -5, 0])
    if k % 512:
        return np.exp2(np.random.permutation(np.resize(levels, k // 32))).repeat(32)
    a = np.empty((k // 512, 16))
    for p in range(k // 512):
        a[p, :8] = np.random.permutation(np.resize(levels, 8))
        for g in range(8):
            far = levels[np.abs(levels - a[p, g]) >= 10]
            a[p, g + 8] = far[np.random.randint(len(far))]
    return np.exp2(a.ravel()).repeat(32)


def f64(x):
    return np.asarray(x).astype(np.float64)


def striped8(idx):
    return np.concatenate([x.reshape(-1, 16).T for x in idx]).astype(np.uint16)


def runs(offs, k):
    lists = np.stack([offs[16 * r : 16 * r + 16].T.reshape(-1) for r in range(8)]).astype(np.int64)
    return lists[np.arange(k) % 512 // 64]


def pack_weight(w):
    k, n = w.shape
    w = f64(np.asarray(w, np.float32).astype(ml_dtypes.bfloat16)).reshape(k // 32, 32, n)
    amax = np.abs(w).max(1)
    byte = np.clip(np.where(amax > 0, np.frexp(amax)[1] - 1 + 127 - 7, 1), 1, 254)
    scaled = (w * np.exp2(127.0 - byte)[:, None, :]).reshape(k, n).astype(np.float32)
    words = np.ascontiguousarray(scaled.reshape(k // 512, 128, 4, n).transpose(0, 1, 3, 2)).astype(ml_dtypes.float8_e4m3fn).view(np.uint8)
    return words, np.ascontiguousarray(byte.astype(np.uint8).reshape(k // 512, 16, n))


def unpack_weight(words, scales):
    g, p, n, _ = words.shape
    vals = np.ascontiguousarray(words).view(ml_dtypes.float8_e4m3fn).astype(np.float64) * np.repeat(np.exp2(scales.astype(np.float64) - 127.0), 8, axis=1)[..., None]
    return vals.transpose(0, 1, 3, 2).reshape(g * 512, n)


E2M1 = np.array([0.0, 0.5, 1.0, 1.5, 2.0, 3.0, 4.0, 6.0, -0.0, -0.5, -1.0, -1.5, -2.0, -3.0, -4.0, -6.0])


def pack_fp4(w):
    k, n = w.shape
    w = f64(np.asarray(w, np.float32).astype(ml_dtypes.bfloat16)).reshape(k // 32, 32, n)
    amax = np.abs(w).max(1)
    mant, ex = np.frexp(amax / 6.0)
    byte = np.clip(np.where(amax > 0, np.where(mant > 0.5, ex, ex - 1) + 127, 1), 1, 254)
    scaled = (w * np.exp2(127.0 - byte)[:, None, :]).reshape(k, n).astype(np.float32)
    c = np.ascontiguousarray(scaled.reshape(k // 512, 128, 4, n).transpose(0, 1, 3, 2)).astype(ml_dtypes.float4_e2m1fn).view(np.uint8) & 0xF
    words = (c[..., 0::2] | (c[..., 1::2] << 4)).reshape(k // 512, 128, 2 * n)
    return np.ascontiguousarray(words), np.ascontiguousarray(byte.astype(np.uint8).reshape(k // 512, 16, n))


def unpack_fp4(words, scales):
    g, _, n = scales.shape
    words = np.ascontiguousarray(words).reshape(g, 128, n, 2)
    nib = np.empty((g, 128, n, 4), np.uint8)
    nib[..., 0::2] = words & 0xF
    nib[..., 1::2] = words >> 4
    vals = E2M1[nib] * np.repeat(np.exp2(scales.astype(np.float64) - 127.0), 8, axis=1)[..., None]
    return vals.transpose(0, 1, 3, 2).reshape(g * 512, n)


K, T, S, H, G, W = 512, 2048, 512, 512, 2048, 256


def setup_inputs():
    n = np.random.standard_normal
    s = mx_kscale(K)[:, None]
    packed_xT = pack_weight(n((K, T)) * s)
    packed_w1 = pack_fp4(n((K, H)) / np.sqrt(K) / s)
    packed_dT = pack_weight(n((K, G)) / s)
    perm = np.stack([np.random.permutation(S) for _ in range(8)])
    return {
        "x_words": packed_xT[0],
        "x_scales": packed_xT[1],
        "w1_words": packed_w1[0],
        "w1_scales": packed_w1[1],
        "gs": (np.random.uniform(0.5, 1.5, (K, 1)) * s).astype(np.float32),
        "d_words": packed_dT[0],
        "d_scales": packed_dT[1],
        "offs": striped8(np.random.randint(0, T, (8, S))),
        "k1": striped8(np.random.randint(0, G, (8, H))),
        "n1": striped8(perm[:, :W]),
        "n2": striped8(perm[:, W:]),
        "n3": striped8(np.stack([np.random.permutation(S) for _ in range(8)])),
    }


def reference(x_words, x_scales, w1_words, w1_scales, gs, d_words, d_scales, offs, k1, n1, n2, n3):
    d_k1 = unpack_weight(d_words, d_scales)[np.arange(K)[:, None], runs(k1, K)]
    xq = unpack_weight(x_words, x_scales)[np.arange(K)[:, None], runs(offs, K)]
    y = unpack_fp4(w1_words, w1_scales).T @ xq
    z = f64(gs) * y
    h = 0.0625 * ((d_k1.T @ mxq(z, 0, "e4m3")))
    pa = h[np.arange(H)[:, None], runs(n1, H)]
    pb = h[np.arange(H)[:, None], runs(n2, H)]
    rb = pa - pb
    ra = pa + pb
    ds = np.zeros((H, S))
    ds[np.arange(H)[:, None], runs(n1, H)] = ra
    dt = ds.copy()
    dt[np.arange(H)[:, None], runs(n2, H)] = rb
    return np.maximum(dt, dt[np.arange(H)[:, None], runs(n3, H)])

@@ -1,0 +1,196 @@
+from contextlib import ExitStack
+
+import concourse.mybir as mybir
+
+F32 = mybir.dt.float32
+BF16 = mybir.dt.bfloat16
+I32 = mybir.dt.int32
+U32 = mybir.dt.uint32
+U16 = mybir.dt.uint16
+U8 = mybir.dt.uint8
+FP8X4 = mybir.dt.float8_e4m3fn_x4
+FP4X4 = mybir.dt.float4_e2m1fn_x4
+COPY = mybir.ActivationFunctionType.Copy
+ADD = mybir.AluOpType.add
+MAX = mybir.AluOpType.max
+
+P = 128
+PACK = 4
+TABLE = 2048
+S = 512
+H = 512
+HALF = S // 2
+PAIRS = S // 2
+FLOPS = 2 * 512 * H * S * 2
+
+
+def tile_picked_hdenseihaarh_none_p_kernel(
+    tc, x_words, x_scales, w1_words, w1_scales, gs, d_words, d_scales, offs, k1, n1, n2, n3, out
+):
+    nc = tc.nc
+    with ExitStack() as ctx:
+        keep = ctx.enter_context(tc.tile_pool(name="keep", bufs=1))
+        psum = ctx.enter_context(tc.psum_pool(name="psum", bufs=1))
+
+        def sb(name, shape, dtype):
+            return keep.tile(shape, dtype, name=name, align_bytes=64)
+
+        def load_list(name, src, cols):
+            tile = keep.tile([P, cols], U16, name=name)
+            nc.sync.dma_start(tile[:], src)
+            return tile
+
+        xs_win = sb("xs_win", [P, TABLE], U8)
+        ds_win = sb("ds_win", [P, TABLE], U8)
+        w1s_raw = sb("w1s_raw", [P, H], U8)
+        xs_plane = sb("xs_plane", [P, S], U8)
+        ds_plane = sb("ds_plane", [P, H], U8)
+        nc.vector.memset(xs_win[:].bitcast(I32), 0)
+        nc.gpsimd.memset(w1s_raw[:].bitcast(I32), 0)
+        nc.vector.memset(ds_win[:].bitcast(I32), 0)
+        nc.vector.memset(xs_plane[:].bitcast(I32), 0)
+        nc.vector.memset(ds_plane[:].bitcast(I32), 0)
+
+        offs_t = load_list("offs_t", offs, S // 16)
+        nc.sync.dma_start(xs_win[:].bitcast(I32)[0:P:8, :], x_scales[0].bitcast(I32))
+        w1_raw = sb("w1_raw", [P, 2 * H], U8)
+        nc.sync.dma_start(w1_raw[:].bitcast(I32), w1_words[0].bitcast(I32))
+        k1_t = load_list("k1_t", k1, H // 16)
+        nc.sync.dma_start(ds_win[:].bitcast(I32)[0:P:8, :], d_scales[0].bitcast(I32))
+        xw_win = sb("xw_win", [P, TABLE], U32)
+        nc.sync.dma_start(xw_win[:].bitcast(I32), x_words[0].rearrange("p n t -> p (n t)").bitcast(I32))
+        dw_win = sb("dw_win", [P, TABLE], U32)
+        nc.sync.dma_start(dw_win[:].bitcast(I32), d_words[0].rearrange("p n t -> p (n t)").bitcast(I32))
+        n1_t = load_list("n1_t", n1, PAIRS // 16)
+        n2_t = load_list("n2_t", n2, PAIRS // 16)
+        n3_t = load_list("n3_t", n3, S // 16)
+
+        for q in range(4):
+            nc.gpsimd.dma_start(
+                w1s_raw[:].bitcast(I32)[32 * q : 32 * q + 4, :], w1_scales[0].bitcast(I32)[4 * q : 4 * q + 4, :]
+            )
+        gs_t = sb("gs_t", [P, PACK], F32)
+        nc.gpsimd.dma_start(gs_t[:], gs.rearrange("(p t) o -> p (t o)", t=PACK))
+
+        def place_rows(plane, src):
+            for r in range(4):
+                nc.scalar.dma_start(plane[:].bitcast(I32)[r:P:32, :], src[:].bitcast(I32)[8 * r : P : 32, :])
+
+        w1_deal = sb("w1_deal", [P, 2 * H], U8)
+        nc.scalar.copy(
+            w1_deal[:].bitcast(U16).rearrange("p (t m) -> p t m", t=PACK),
+            w1_raw[:].bitcast(U16).rearrange("p (m t) -> p t m", t=PACK),
+        )
+
+        xs_pick = sb("xs_pick", [P, S], U8)
+        nc.vector.tensor_copy(xs_pick[:], xs_win[:].indirect(offs_t[:]))
+        place_rows(xs_plane, xs_pick)
+
+        w1s_deal = sb("w1s_deal", [P, H], U8)
+        nc.vector.tensor_copy(
+            w1s_deal[:].rearrange("p (t m) -> p t m", t=PACK), w1s_raw[:].rearrange("p (m t) -> p t m", t=PACK)
+        )
+
+        xw_pick = [sb("xw_pick%d" % c, [P, HALF], U32) for c in range(2)]
+        for c in range(2):
+            nc.vector.tensor_copy(xw_pick[c][:], xw_win[:].indirect(offs_t[:, 16 * c : 16 * c + 16]))
+
+        ds_pick = sb("ds_pick", [P, H], U8)
+        nc.vector.tensor_copy(ds_pick[:], ds_win[:].indirect(k1_t[:]))
+        ds_deal = sb("ds_deal", [P, H], U8)
+        nc.vector.tensor_copy(
+            ds_deal[:].rearrange("p (t m) -> p t m", t=PACK), ds_pick[:].rearrange("p (m t) -> p t m", t=PACK)
+        )
+        place_rows(ds_plane, ds_deal)
+
+        z_planes = [sb("z_planes%d" % c, [P, PACK, HALF], BF16) for c in range(2)]
+        for c in range(2):
+            cols = slice(c * HALF, (c + 1) * HALF)
+            for u in range(2):
+                y_bank = psum.tile([P, 2, HALF], F32, name="y_bank%d%d" % (c, u))
+                for a in range(2):
+                    t = 2 * u + a
+                    nc.tensor.matmul_mx(
+                        out=y_bank[:, a, :],
+                        lhsT=w1_deal[:, 2 * P * t : 2 * P * (t + 1)].bitcast(FP4X4),
+                        lhsT_scale=w1s_deal[:, P * t : P * (t + 1)],
+                        rhs=xw_pick[c][:].bitcast(FP8X4),
+                        rhs_scale=xs_plane[:, cols],
+                        start=True,
+                        stop=True,
+                    )
+                for a in range(2):
+                    t = 2 * u + a
+                    nc.scalar.activation(z_planes[c][:, t, :], y_bank[:, a, :], COPY, scale=gs_t[:, t : t + 1])
+
+        dw_pick = sb("dw_pick", [P, H], U32)
+        nc.vector.tensor_copy(dw_pick[:], dw_win[:].indirect(k1_t[:]))
+        dw_deal = sb("dw_deal", [P, H], U32)
+        nc.vector.tensor_copy(
+            dw_deal[:].rearrange("p (t m) -> p t m", t=PACK), dw_pick[:].rearrange("p (m t) -> p t m", t=PACK)
+        )
+
+        z_codes = [sb("z_codes%d" % c, [P, HALF], U32) for c in range(2)]
+        z_scales = [sb("z_scales%d" % c, [P, HALF], U8) for c in range(2)]
+        z_rows = [sb("z_rows%d" % c, [P, HALF, PACK], BF16) for c in range(2)]
+        for c in range(2):
+            nc.vector.tensor_copy(
+                z_rows[c][:].rearrange("p (c i) t -> p c t i", i=4),
+                z_planes[c][:].rearrange("p t (c i) -> p c t i", i=4),
+            )
+            nc.vector.quantize_mx(
+                out=z_codes[c][:].bitcast(FP8X4),
+                scales=z_scales[c][:],
+                in_=z_rows[c][:].rearrange("p n t -> p (n t)"),
+            )
+
+        h_banks = [psum.tile([P, S], F32, name="h_bank%d" % t) for t in range(PACK)]
+        for c in range(2):
+            for t in range(PACK):
+                nc.tensor.matmul_mx(
+                    out=h_banks[t][:, c * HALF : (c + 1) * HALF],
+                    lhsT=dw_deal[:, P * t : P * (t + 1)].bitcast(FP8X4),
+                    lhsT_scale=ds_plane[:, P * t : P * (t + 1)],
+                    rhs=z_codes[c][:].bitcast(FP8X4),
+                    rhs_scale=z_scales[c][:],
+                    start=True,
+                    stop=True,
+                )
+
+        out_rows = out.rearrange("(p t) j -> p t j", t=PACK)
+        dt = [sb("dt%d" % t, [P, S], F32) for t in range(PACK)]
+        pa = [sb("pa%d" % t, [P, PAIRS], F32) for t in range(PACK)]
+        pb = [sb("pb%d" % t, [P, PAIRS], F32) for t in range(PACK)]
+        nb = [sb("nb%d" % t, [P, PAIRS], F32) for t in range(PACK)]
+
+        def fetch_pairs(t):
+            h = sb("h%d" % t, [P, S], F32)
+            nc.scalar.activation(h[:], h_banks[t][:], COPY, scale=0.0625)
+            nc.scalar.activation(pa[t][:], h[:].indirect(n1_t[:]), COPY)
+            nc.scalar.activation(pb[t][:], h[:].indirect(n2_t[:]), COPY)
+            nc.scalar.activation(nb[t][:], pb[t][:], COPY, scale=-1.0)
+
+        def put_sums(t):
+            nc.vector.tensor_tensor(dt[t][:].indirect(n1_t[:]), pa[t][:], pb[t][:], ADD)
+
+        def put_differences(t):
+            nc.vector.tensor_tensor(dt[t][:].indirect(n2_t[:]), pa[t][:], nb[t][:], ADD)
+
+        def finish(t):
+            other = sb("other%d" % t, [P, S], F32)
+            res = sb("res%d" % t, [P, S], F32)
+            for c in range(2):
+                cols = slice(c * HALF, (c + 1) * HALF)
+                nc.scalar.activation(other[:, cols], dt[t][:].indirect(n3_t[:, 16 * c : 16 * c + 16]), COPY)
+            nc.vector.tensor_tensor(res[:], dt[t][:], other[:], MAX)
+            nc.sync.dma_start(out_rows[:, t, :], res[:])
+
+        fetch_pairs(0)
+        for t in range(PACK):
+            put_sums(t)
+            if t + 1 < PACK:
+                fetch_pairs(t + 1)
+            if t > 0:
+                finish(t - 1)
+            put_differences(t)
+        finish(PACK - 1)

@@ -40,41 +40,39 @@ def tile_picked_hdenseihaarh_none_p_kernel(
             nc.sync.dma_start(tile[:], src)
             return tile
 
-        xs_win = sb("xs_win", [P, TABLE], U8)
+        xs_win = keep.tile([P, TABLE], U8, name="xs_win", tag="xs_then_dw", align_bytes=64)
         ds_win = sb("ds_win", [P, TABLE], U8)
         w1s_raw = sb("w1s_raw", [P, H], U8)
         xs_plane = sb("xs_plane", [P, S], U8)
         ds_plane = sb("ds_plane", [P, H], U8)
         nc.vector.memset(xs_win[:].bitcast(I32), 0)
-        nc.gpsimd.memset(w1s_raw[:].bitcast(I32), 0)
+        nc.vector.memset(w1s_raw[:].bitcast(I32), 0)
         nc.vector.memset(ds_win[:].bitcast(I32), 0)
-        nc.vector.memset(xs_plane[:].bitcast(I32), 0)
-        nc.vector.memset(ds_plane[:].bitcast(I32), 0)
+        nc.gpsimd.memset(xs_plane[:].bitcast(I32), 0)
+        nc.gpsimd.memset(ds_plane[:].bitcast(I32), 0)
 
         offs_t = load_list("offs_t", offs, S // 16)
-        nc.sync.dma_start(xs_win[:].bitcast(I32)[0:P:8, :], x_scales[0].bitcast(I32))
-        w1_raw = sb("w1_raw", [P, 2 * H], U8)
-        nc.sync.dma_start(w1_raw[:].bitcast(I32), w1_words[0].bitcast(I32))
         k1_t = load_list("k1_t", k1, H // 16)
-        nc.sync.dma_start(ds_win[:].bitcast(I32)[0:P:8, :], d_scales[0].bitcast(I32))
         xw_win = sb("xw_win", [P, TABLE], U32)
         nc.sync.dma_start(xw_win[:].bitcast(I32), x_words[0].rearrange("p n t -> p (n t)").bitcast(I32))
-        dw_win = sb("dw_win", [P, TABLE], U32)
-        nc.sync.dma_start(dw_win[:].bitcast(I32), d_words[0].rearrange("p n t -> p (n t)").bitcast(I32))
         n1_t = load_list("n1_t", n1, PAIRS // 16)
         n2_t = load_list("n2_t", n2, PAIRS // 16)
         n3_t = load_list("n3_t", n3, S // 16)
 
+        w1_raw = sb("w1_raw", [P, 2 * H], U8)
+        nc.scalar.dma_start(w1_raw[:].bitcast(I32), w1_words[0].bitcast(I32))
+        nc.scalar.dma_start(xs_win[:].bitcast(I32)[0:P:8, :], x_scales[0].bitcast(I32))
         for q in range(4):
-            nc.gpsimd.dma_start(
+            nc.scalar.dma_start(
                 w1s_raw[:].bitcast(I32)[32 * q : 32 * q + 4, :], w1_scales[0].bitcast(I32)[4 * q : 4 * q + 4, :]
             )
+        nc.scalar.dma_start(ds_win[:].bitcast(I32)[0:P:8, :], d_scales[0].bitcast(I32))
         gs_t = sb("gs_t", [P, PACK], F32)
-        nc.gpsimd.dma_start(gs_t[:], gs.rearrange("(p t) o -> p (t o)", t=PACK))
+        nc.scalar.dma_start(gs_t[:], gs.rearrange("(p t) o -> p (t o)", t=PACK))
 
         def place_rows(plane, src):
             for r in range(4):
-                nc.scalar.dma_start(plane[:].bitcast(I32)[r:P:32, :], src[:].bitcast(I32)[8 * r : P : 32, :])
+                nc.sync.dma_start(plane[:].bitcast(I32)[r:P:32, :], src[:].bitcast(I32)[8 * r : P : 32, :])
 
         w1_deal = sb("w1_deal", [P, 2 * H], U8)
         nc.scalar.copy(
@@ -85,6 +83,8 @@ def tile_picked_hdenseihaarh_none_p_kernel(
         xs_pick = sb("xs_pick", [P, S], U8)
         nc.vector.tensor_copy(xs_pick[:], xs_win[:].indirect(offs_t[:]))
         place_rows(xs_plane, xs_pick)
+        dw_win = keep.tile([P, TABLE], U32, name="dw_win", tag="xs_then_dw", align_bytes=64)
+        nc.sync.dma_start(dw_win[:].bitcast(I32), d_words[0].rearrange("p n t -> p (n t)").bitcast(I32))
 
         w1s_deal = sb("w1s_deal", [P, H], U8)
         nc.vector.tensor_copy(
@@ -144,11 +144,12 @@ def tile_picked_hdenseihaarh_none_p_kernel(
                 in_=z_rows[c][:].rearrange("p n t -> p (n t)"),
             )
 
+        h_first = psum.tile([P, 2, HALF], F32, name="h_first", tag="y_bank00")
         h_banks = [psum.tile([P, S], F32, name="h_bank%d" % t) for t in range(PACK)]
         for c in range(2):
             for t in range(PACK):
                 nc.tensor.matmul_mx(
-                    out=h_banks[t][:, c * HALF : (c + 1) * HALF],
+                    out=h_first[:, 0, :] if (c, t) == (0, 0) else h_banks[t][:, c * HALF : (c + 1) * HALF],
                     lhsT=dw_deal[:, P * t : P * (t + 1)].bitcast(FP8X4),
                     lhsT_scale=ds_plane[:, P * t : P * (t + 1)],
                     rhs=z_codes[c][:].bitcast(FP8X4),
@@ -159,38 +160,42 @@ def tile_picked_hdenseihaarh_none_p_kernel(
 
         out_rows = out.rearrange("(p t) j -> p t j", t=PACK)
         dt = [sb("dt%d" % t, [P, S], F32) for t in range(PACK)]
-        pa = [sb("pa%d" % t, [P, PAIRS], F32) for t in range(PACK)]
-        pb = [sb("pb%d" % t, [P, PAIRS], F32) for t in range(PACK)]
-        nb = [sb("nb%d" % t, [P, PAIRS], F32) for t in range(PACK)]
 
-        def fetch_pairs(t):
+        def pair_up(t):
             h = sb("h%d" % t, [P, S], F32)
-            nc.scalar.activation(h[:], h_banks[t][:], COPY, scale=0.0625)
-            nc.scalar.activation(pa[t][:], h[:].indirect(n1_t[:]), COPY)
-            nc.scalar.activation(pb[t][:], h[:].indirect(n2_t[:]), COPY)
-            nc.scalar.activation(nb[t][:], pb[t][:], COPY, scale=-1.0)
+            pa = sb("pa%d" % t, [P, PAIRS], F32)
+            pb = sb("pb%d" % t, [P, PAIRS], F32)
+            nb = sb("nb%d" % t, [P, PAIRS], F32)
+            if t == 0:
+                nc.scalar.activation(h[:, :HALF], h_first[:, 0, :], COPY, scale=0.0625)
+                nc.scalar.activation(h[:, HALF:], h_banks[t][:, HALF:], COPY, scale=0.0625)
+                nc.vector.tensor_copy(pa[:], h[:].indirect(n1_t[:]))
+            else:
+                nc.scalar.activation(h[:], h_banks[t][:], COPY, scale=0.0625)
+                nc.scalar.activation(pa[:], h[:].indirect(n1_t[:]), COPY)
+            nc.scalar.activation(pb[:], h[:].indirect(n2_t[:]), COPY)
+            nc.scalar.activation(nb[:], pb[:], COPY, scale=-1.0)
+            nc.vector.tensor_tensor(dt[t][:].indirect(n1_t[:]), pa[:], pb[:], ADD)
+            nc.vector.tensor_tensor(dt[t][:].indirect(n2_t[:]), pa[:], nb[:], ADD)
 
-        def put_sums(t):
-            nc.vector.tensor_tensor(dt[t][:].indirect(n1_t[:]), pa[t][:], pb[t][:], ADD)
-
-        def put_differences(t):
-            nc.vector.tensor_tensor(dt[t][:].indirect(n2_t[:]), pa[t][:], nb[t][:], ADD)
-
-        def finish(t):
+        def finish(t, fetch_widths, store_widths):
             other = sb("other%d" % t, [P, S], F32)
             res = sb("res%d" % t, [P, S], F32)
-            for c in range(2):
-                cols = slice(c * HALF, (c + 1) * HALF)
-                nc.scalar.activation(other[:, cols], dt[t][:].indirect(n3_t[:, 16 * c : 16 * c + 16]), COPY)
-            nc.vector.tensor_tensor(res[:], dt[t][:], other[:], MAX)
-            nc.sync.dma_start(out_rows[:, t, :], res[:])
+            lo = 0
+            for w in fetch_widths:
+                nc.scalar.activation(
+                    other[:, lo : lo + w], dt[t][:].indirect(n3_t[:, lo // 16 : (lo + w) // 16]), COPY
+                )
+                lo = lo + w
+            lo = 0
+            for w in store_widths:
+                cols = slice(lo, lo + w)
+                nc.vector.tensor_tensor(res[:, cols], dt[t][:, cols], other[:, cols], MAX)
+                nc.sync.dma_start(out_rows[:, t, cols], res[:, cols])
+                lo = lo + w
 
-        fetch_pairs(0)
-        for t in range(PACK):
-            put_sums(t)
-            if t + 1 < PACK:
-                fetch_pairs(t + 1)
-            if t > 0:
-                finish(t - 1)
-            put_differences(t)
-        finish(PACK - 1)
+        pair_up(0)
+        for t in range(1, PACK):
+            pair_up(t)
+            finish(t - 1, [256, 256], [512])
+        finish(PACK - 1, [256, 128, 128], [256, 128, 128])

@@ -12,6 +12,7 @@ FP8X4 = mybir.dt.float8_e4m3fn_x4
 FP4X4 = mybir.dt.float4_e2m1fn_x4
 COPY = mybir.ActivationFunctionType.Copy
 ADD = mybir.AluOpType.add
+MULT = mybir.AluOpType.mult
 MAX = mybir.AluOpType.max
 
 P = 128
@@ -40,38 +41,39 @@ def tile_picked_hdenseihaarh_none_p_kernel(
             nc.sync.dma_start(tile[:], src)
             return tile
 
-        xs_win = keep.tile([P, TABLE], U8, name="xs_win", tag="xs_then_dw", align_bytes=64)
+        xs_win = sb("xs_win", [P, TABLE], U8)
         ds_win = sb("ds_win", [P, TABLE], U8)
         w1s_raw = sb("w1s_raw", [P, H], U8)
         xs_plane = sb("xs_plane", [P, S], U8)
         ds_plane = sb("ds_plane", [P, H], U8)
-        nc.vector.memset(xs_win[:].bitcast(I32), 0)
-        nc.vector.memset(w1s_raw[:].bitcast(I32), 0)
         nc.vector.memset(ds_win[:].bitcast(I32), 0)
-        nc.gpsimd.memset(xs_plane[:].bitcast(I32), 0)
-        nc.gpsimd.memset(ds_plane[:].bitcast(I32), 0)
+        nc.vector.memset(ds_plane[:].bitcast(I32), 0)
 
         offs_t = load_list("offs_t", offs, S // 16)
+        nc.sync.dma_start(
+            xs_win[:].bitcast(I32), x_scales[0].bitcast(I32).unsqueeze(1).to_broadcast([16, 8, TABLE // 4])
+        )
         k1_t = load_list("k1_t", k1, H // 16)
+        nc.sync.dma_start(ds_win[:].bitcast(I32)[0:P:8, :], d_scales[0].bitcast(I32))
         xw_win = sb("xw_win", [P, TABLE], U32)
         nc.sync.dma_start(xw_win[:].bitcast(I32), x_words[0].rearrange("p n t -> p (n t)").bitcast(I32))
+        for r in range(4):
+            nc.sync.dma_start(
+                w1s_raw[:].bitcast(I32)[r:P:4, :],
+                w1_scales[0].bitcast(I32)[r:16:4, :].unsqueeze(1).to_broadcast([4, 8, H // 4]),
+            )
+        w1_raw = sb("w1_raw", [P, 2 * H], U8)
+        nc.sync.dma_start(w1_raw[:].bitcast(I32), w1_words[0].bitcast(I32))
+        dw_win = keep.tile([P, TABLE], U32, name="dw_win", tag="dw_win_then_z", align_bytes=64)
+        nc.sync.dma_start(dw_win[:].bitcast(I32), d_words[0].rearrange("p n t -> p (n t)").bitcast(I32))
+        gs_t = sb("gs_t", [P, PACK], F32)
+        nc.sync.dma_start(gs_t[:], gs.rearrange("(p t) o -> p (t o)", t=PACK))
         n1_t = load_list("n1_t", n1, PAIRS // 16)
         n2_t = load_list("n2_t", n2, PAIRS // 16)
         n3_t = load_list("n3_t", n3, S // 16)
 
-        w1_raw = sb("w1_raw", [P, 2 * H], U8)
-        nc.scalar.dma_start(w1_raw[:].bitcast(I32), w1_words[0].bitcast(I32))
-        nc.scalar.dma_start(xs_win[:].bitcast(I32)[0:P:8, :], x_scales[0].bitcast(I32))
-        for q in range(4):
-            nc.scalar.dma_start(
-                w1s_raw[:].bitcast(I32)[32 * q : 32 * q + 4, :], w1_scales[0].bitcast(I32)[4 * q : 4 * q + 4, :]
-            )
-        nc.scalar.dma_start(ds_win[:].bitcast(I32)[0:P:8, :], d_scales[0].bitcast(I32))
-        gs_t = sb("gs_t", [P, PACK], F32)
-        nc.scalar.dma_start(gs_t[:], gs.rearrange("(p t) o -> p (t o)", t=PACK))
-
-        def place_rows(plane, src):
-            for r in range(4):
+        def place_rows(plane, src, rows):
+            for r in rows:
                 nc.sync.dma_start(plane[:].bitcast(I32)[r:P:32, :], src[:].bitcast(I32)[8 * r : P : 32, :])
 
         w1_deal = sb("w1_deal", [P, 2 * H], U8)
@@ -82,9 +84,16 @@ def tile_picked_hdenseihaarh_none_p_kernel(
 
         xs_pick = sb("xs_pick", [P, S], U8)
         nc.vector.tensor_copy(xs_pick[:], xs_win[:].indirect(offs_t[:]))
-        place_rows(xs_plane, xs_pick)
-        dw_win = keep.tile([P, TABLE], U32, name="dw_win", tag="xs_then_dw", align_bytes=64)
-        nc.sync.dma_start(dw_win[:].bitcast(I32), d_words[0].rearrange("p n t -> p (n t)").bitcast(I32))
+        nc.vector.tensor_copy(xs_plane[:].bitcast(I32), xs_pick[:].bitcast(I32))
+        place_rows(xs_plane, xs_pick, range(1, 4))
+
+        ds_pick = keep.tile([P, H], U8, name="ds_pick", tag="dw_then_z", align_bytes=64)
+        nc.vector.tensor_copy(ds_pick[:], ds_win[:].indirect(k1_t[:]))
+        ds_deal = sb("ds_deal", [P, H], U8)
+        nc.vector.tensor_copy(
+            ds_deal[:].rearrange("p (t m) -> p t m", t=PACK), ds_pick[:].rearrange("p (m t) -> p t m", t=PACK)
+        )
+        place_rows(ds_plane, ds_deal, range(4))
 
         w1s_deal = sb("w1s_deal", [P, H], U8)
         nc.vector.tensor_copy(
@@ -95,107 +104,162 @@ def tile_picked_hdenseihaarh_none_p_kernel(
         for c in range(2):
             nc.vector.tensor_copy(xw_pick[c][:], xw_win[:].indirect(offs_t[:, 16 * c : 16 * c + 16]))
 
-        ds_pick = sb("ds_pick", [P, H], U8)
-        nc.vector.tensor_copy(ds_pick[:], ds_win[:].indirect(k1_t[:]))
-        ds_deal = sb("ds_deal", [P, H], U8)
-        nc.vector.tensor_copy(
-            ds_deal[:].rearrange("p (t m) -> p t m", t=PACK), ds_pick[:].rearrange("p (m t) -> p t m", t=PACK)
-        )
-        place_rows(ds_plane, ds_deal)
-
-        z_planes = [sb("z_planes%d" % c, [P, PACK, HALF], BF16) for c in range(2)]
-        for c in range(2):
-            cols = slice(c * HALF, (c + 1) * HALF)
-            for u in range(2):
-                y_bank = psum.tile([P, 2, HALF], F32, name="y_bank%d%d" % (c, u))
-                for a in range(2):
-                    t = 2 * u + a
-                    nc.tensor.matmul_mx(
-                        out=y_bank[:, a, :],
-                        lhsT=w1_deal[:, 2 * P * t : 2 * P * (t + 1)].bitcast(FP4X4),
-                        lhsT_scale=w1s_deal[:, P * t : P * (t + 1)],
-                        rhs=xw_pick[c][:].bitcast(FP8X4),
-                        rhs_scale=xs_plane[:, cols],
-                        start=True,
-                        stop=True,
-                    )
-                for a in range(2):
-                    t = 2 * u + a
-                    nc.scalar.activation(z_planes[c][:, t, :], y_bank[:, a, :], COPY, scale=gs_t[:, t : t + 1])
-
-        dw_pick = sb("dw_pick", [P, H], U32)
-        nc.vector.tensor_copy(dw_pick[:], dw_win[:].indirect(k1_t[:]))
-        dw_deal = sb("dw_deal", [P, H], U32)
-        nc.vector.tensor_copy(
-            dw_deal[:].rearrange("p (t m) -> p t m", t=PACK), dw_pick[:].rearrange("p (m t) -> p t m", t=PACK)
-        )
-
-        z_codes = [sb("z_codes%d" % c, [P, HALF], U32) for c in range(2)]
-        z_scales = [sb("z_scales%d" % c, [P, HALF], U8) for c in range(2)]
-        z_rows = [sb("z_rows%d" % c, [P, HALF, PACK], BF16) for c in range(2)]
-        for c in range(2):
-            nc.vector.tensor_copy(
-                z_rows[c][:].rearrange("p (c i) t -> p c t i", i=4),
-                z_planes[c][:].rearrange("p t (c i) -> p c t i", i=4),
+        def first_product(out_ap, t, lo, width):
+            c = lo // HALF
+            nc.tensor.matmul_mx(
+                out=out_ap,
+                lhsT=w1_deal[:, 2 * P * t : 2 * P * (t + 1)].bitcast(FP4X4),
+                lhsT_scale=w1s_deal[:, P * t : P * (t + 1)],
+                rhs=xw_pick[c][:, lo - c * HALF : lo - c * HALF + width].bitcast(FP8X4),
+                rhs_scale=xs_plane[:, lo : lo + width],
+                start=True,
+                stop=True,
             )
+
+        z_planes = sb("z_planes", [P, PACK, HALF], BF16)
+        for u in range(2):
+            y_bank = psum.tile([P, 2, HALF], F32, name="y_bank0%d" % u)
+            for a in range(2):
+                first_product(y_bank[:, a, :], 2 * u + a, 0, HALF)
+            for a in range(2):
+                t = 2 * u + a
+                nc.scalar.activation(z_planes[:, t, :], y_bank[:, a, :], COPY, scale=gs_t[:, t : t + 1])
+        y_quads = [psum.tile([P, PACK, P], F32, name="y_bank1%d" % u) for u in range(2)]
+        for u in range(2):
+            for t in range(PACK):
+                first_product(y_quads[u][:, t, :], t, HALF + u * P, P)
+
+        dw_pick = keep.tile([P, H], U32, name="dw_pick", tag="dw_then_z", align_bytes=64)
+        nc.vector.tensor_copy(dw_pick[:], dw_win[:].indirect(k1_t[:]))
+        dw_deal = sb("dw_deal", [P, PACK, P], U32)
+        dw_by_tile = dw_pick[:].rearrange("p (m t) -> p t m", t=PACK)
+        nc.vector.tensor_copy(dw_deal[:, 0, :], dw_by_tile[:, 0, :])
+
+        z_rows = [
+            sb("z_rows0", [P, HALF, PACK], BF16),
+            keep.tile([P, HALF, PACK], BF16, name="z_rows1", tag="dw_win_then_z", align_bytes=64),
+        ]
+        z_codes = sb("z_codes", [P, S], U32)
+        z_scales = sb("z_scales", [P, S], U8)
+
+        def quantise(c):
             nc.vector.quantize_mx(
-                out=z_codes[c][:].bitcast(FP8X4),
-                scales=z_scales[c][:],
+                out=z_codes[:, c * HALF : (c + 1) * HALF].bitcast(FP8X4),
+                scales=z_scales[:, c * HALF : (c + 1) * HALF],
                 in_=z_rows[c][:].rearrange("p n t -> p (n t)"),
             )
 
-        h_first = psum.tile([P, 2, HALF], F32, name="h_first", tag="y_bank00")
-        h_banks = [psum.tile([P, S], F32, name="h_bank%d" % t) for t in range(PACK)]
-        for c in range(2):
-            for t in range(PACK):
-                nc.tensor.matmul_mx(
-                    out=h_first[:, 0, :] if (c, t) == (0, 0) else h_banks[t][:, c * HALF : (c + 1) * HALF],
-                    lhsT=dw_deal[:, P * t : P * (t + 1)].bitcast(FP8X4),
-                    lhsT_scale=ds_plane[:, P * t : P * (t + 1)],
-                    rhs=z_codes[c][:].bitcast(FP8X4),
-                    rhs_scale=z_scales[c][:],
-                    start=True,
-                    stop=True,
-                )
+        for u in range(2):
+            nc.vector.tensor_tensor(
+                z_rows[1][:, u * P : (u + 1) * P, :],
+                y_quads[u][:].rearrange("p t n -> p n t"),
+                gs_t[:].unsqueeze(1).to_broadcast([P, P, PACK]),
+                MULT,
+            )
+        nc.scalar.copy(
+            z_rows[0][:, :P, :].rearrange("p (c i) t -> p c t i", i=4),
+            z_planes[:, :, :P].rearrange("p t (c i) -> p c t i", i=4),
+        )
+        nc.vector.tensor_copy(
+            z_rows[0][:, P:, :].rearrange("p (c i) t -> p c t i", i=4),
+            z_planes[:, :, P:].rearrange("p t (c i) -> p c t i", i=4),
+        )
+        quantise(1)
+        quantise(0)
+        nc.vector.tensor_copy(dw_deal[:, 1:, :], dw_by_tile[:, 1:, :])
+
+        h_first = psum.tile([P, 2, HALF], F32, name="h_first", tag="y_bank10")
+        h_banks = {}
+
+        def second_product(out_ap, t, cols):
+            nc.tensor.matmul_mx(
+                out=out_ap,
+                lhsT=dw_deal[:, t, :].bitcast(FP8X4),
+                lhsT_scale=ds_plane[:, P * t : P * (t + 1)],
+                rhs=z_codes[:, cols].bitcast(FP8X4),
+                rhs_scale=z_scales[:, cols],
+                start=True,
+                stop=True,
+            )
+
+        def whole_product(t):
+            h_banks[t] = psum.tile([P, S], F32, name="h_bank%d" % t, tag="h_bank%d" % (t % 2))
+            second_product(h_banks[t][:], t, slice(0, S))
+
+        h_banks[0] = psum.tile([P, S], F32, name="h_bank0", tag="h_bank0")
+        second_product(h_first[:, 0, :], 0, slice(HALF, S))
+        second_product(h_banks[0][:, :HALF], 0, slice(0, HALF))
+        whole_product(1)
 
         out_rows = out.rearrange("(p t) j -> p t j", t=PACK)
         dt = [sb("dt%d" % t, [P, S], F32) for t in range(PACK)]
+        h = {}
+        pa = [sb("pa%d" % t, [P, PAIRS], F32) for t in range(PACK)]
+        nb = [sb("nb%d" % t, [P, PAIRS], F32) for t in range(PACK)]
+        pb = [
+            keep.tile([P, PAIRS], F32, name="pb%d" % t, tag="pb_then_res%d" % t, align_bytes=64) for t in range(PACK)
+        ]
+        other = {}
 
-        def pair_up(t):
-            h = sb("h%d" % t, [P, S], F32)
-            pa = sb("pa%d" % t, [P, PAIRS], F32)
-            pb = sb("pb%d" % t, [P, PAIRS], F32)
-            nb = sb("nb%d" % t, [P, PAIRS], F32)
+        def new_h(t):
+            h[t] = keep.tile([P, S], F32, name="h%d" % t, tag="h_then_other%d" % max(t, 1), align_bytes=64)
+
+        def leave_psum(t):
+            new_h(t)
+            nc.scalar.activation(h[t][:], h_banks[t][:], COPY, scale=0.0625)
+
+        def fetch_pairs(t):
             if t == 0:
-                nc.scalar.activation(h[:, :HALF], h_first[:, 0, :], COPY, scale=0.0625)
-                nc.scalar.activation(h[:, HALF:], h_banks[t][:, HALF:], COPY, scale=0.0625)
-                nc.vector.tensor_copy(pa[:], h[:].indirect(n1_t[:]))
+                nc.vector.tensor_copy(pa[t][:], h[t][:].indirect(n1_t[:]))
             else:
-                nc.scalar.activation(h[:], h_banks[t][:], COPY, scale=0.0625)
-                nc.scalar.activation(pa[:], h[:].indirect(n1_t[:]), COPY)
-            nc.scalar.activation(pb[:], h[:].indirect(n2_t[:]), COPY)
-            nc.scalar.activation(nb[:], pb[:], COPY, scale=-1.0)
-            nc.vector.tensor_tensor(dt[t][:].indirect(n1_t[:]), pa[:], pb[:], ADD)
-            nc.vector.tensor_tensor(dt[t][:].indirect(n2_t[:]), pa[:], nb[:], ADD)
+                nc.scalar.activation(pa[t][:], h[t][:].indirect(n1_t[:]), COPY)
+            nc.scalar.activation(pb[t][:], h[t][:].indirect(n2_t[:]), COPY)
+            nc.scalar.activation(nb[t][:], pb[t][:], COPY, scale=-1.0)
 
-        def finish(t, fetch_widths, store_widths):
-            other = sb("other%d" % t, [P, S], F32)
-            res = sb("res%d" % t, [P, S], F32)
+        def put_sums(t):
+            nc.vector.tensor_tensor(dt[t][:].indirect(n1_t[:]), pa[t][:], pb[t][:], ADD)
+
+        def put_differences(t):
+            nc.vector.tensor_tensor(dt[t][:].indirect(n2_t[:]), pa[t][:], nb[t][:], ADD)
+
+        def fetch_other(t, widths):
+            other[t] = keep.tile([P, S], F32, name="other%d" % t, tag="h_then_other%d" % (t + 1), align_bytes=64)
             lo = 0
-            for w in fetch_widths:
+            for w in widths:
                 nc.scalar.activation(
-                    other[:, lo : lo + w], dt[t][:].indirect(n3_t[:, lo // 16 : (lo + w) // 16]), COPY
+                    other[t][:, lo : lo + w], dt[t][:].indirect(n3_t[:, lo // 16 : (lo + w) // 16]), COPY
                 )
                 lo = lo + w
+
+        def finish(t, widths):
+            res = keep.tile([P, S], F32, name="res%d" % t, tag="pb_then_res%d" % (t + 2), align_bytes=64)
             lo = 0
-            for w in store_widths:
+            for w in widths:
                 cols = slice(lo, lo + w)
-                nc.vector.tensor_tensor(res[:, cols], dt[t][:, cols], other[:, cols], MAX)
+                nc.vector.tensor_tensor(res[:, cols], dt[t][:, cols], other[t][:, cols], MAX)
                 nc.sync.dma_start(out_rows[:, t, cols], res[:, cols])
                 lo = lo + w
 
-        pair_up(0)
-        for t in range(1, PACK):
-            pair_up(t)
-            finish(t - 1, [256, 256], [512])
-        finish(PACK - 1, [256, 128, 128], [256, 128, 128])
+        new_h(0)
+        nc.scalar.activation(h[0][:, HALF:], h_first[:, 0, :], COPY, scale=0.0625)
+        nc.scalar.activation(h[0][:, :HALF], h_banks[0][:, :HALF], COPY, scale=0.0625)
+        fetch_pairs(0)
+        put_sums(0)
+        put_differences(0)
+        leave_psum(1)
+        fetch_pairs(1)
+        put_sums(1)
+        put_differences(1)
+        for t in range(2, PACK):
+            whole_product(t)
+            leave_psum(t)
+        for t in range(2, PACK):
+            fetch_other(t - 2, [256, 256])
+            fetch_pairs(t)
+            put_sums(t)
+            finish(t - 2, [512])
+            put_differences(t)
+        fetch_other(2, [256, 256])
+        finish(2, [512])
+        fetch_other(3, [256, 128, 128])
+        finish(3, [256, 128, 128])

from contextlib import ExitStack

import concourse.mybir as mybir

F32 = mybir.dt.float32
BF16 = mybir.dt.bfloat16
I32 = mybir.dt.int32
U32 = mybir.dt.uint32
U16 = mybir.dt.uint16
U8 = mybir.dt.uint8
FP8X4 = mybir.dt.float8_e4m3fn_x4
FP4X4 = mybir.dt.float4_e2m1fn_x4
COPY = mybir.ActivationFunctionType.Copy
ADD = mybir.AluOpType.add
MULT = mybir.AluOpType.mult
MAX = mybir.AluOpType.max

P = 128
PACK = 4
TABLE = 2048
S = 512
H = 512
HALF = S // 2
PAIRS = S // 2
FLOPS = 2 * 512 * H * S * 2


def tile_picked_hdenseihaarh_none_p_kernel(
    tc, x_words, x_scales, w1_words, w1_scales, gs, d_words, d_scales, offs, k1, n1, n2, n3, out
):
    nc = tc.nc
    with ExitStack() as ctx:
        keep = ctx.enter_context(tc.tile_pool(name="keep", bufs=1))
        psum = ctx.enter_context(tc.psum_pool(name="psum", bufs=1))

        def sb(name, shape, dtype):
            return keep.tile(shape, dtype, name=name, align_bytes=64)

        def load_list(name, src, cols):
            tile = keep.tile([P, cols], U16, name=name)
            nc.sync.dma_start(tile[:], src)
            return tile

        xs_win = sb("xs_win", [P, TABLE], U8)
        ds_win = sb("ds_win", [P, TABLE], U8)
        w1s_raw = sb("w1s_raw", [P, H], U8)
        xs_plane = sb("xs_plane", [P, S], U8)
        ds_plane = sb("ds_plane", [P, H], U8)
        nc.vector.memset(ds_win[:].bitcast(I32), 0)
        nc.vector.memset(ds_plane[:].bitcast(I32), 0)

        offs_t = load_list("offs_t", offs, S // 16)
        nc.sync.dma_start(
            xs_win[:].bitcast(I32), x_scales[0].bitcast(I32).unsqueeze(1).to_broadcast([16, 8, TABLE // 4])
        )
        k1_t = load_list("k1_t", k1, H // 16)
        nc.sync.dma_start(ds_win[:].bitcast(I32)[0:P:8, :], d_scales[0].bitcast(I32))
        xw_win = sb("xw_win", [P, TABLE], U32)
        nc.sync.dma_start(xw_win[:].bitcast(I32), x_words[0].rearrange("p n t -> p (n t)").bitcast(I32))
        for r in range(4):
            nc.sync.dma_start(
                w1s_raw[:].bitcast(I32)[r:P:4, :],
                w1_scales[0].bitcast(I32)[r:16:4, :].unsqueeze(1).to_broadcast([4, 8, H // 4]),
            )
        w1_raw = sb("w1_raw", [P, 2 * H], U8)
        nc.sync.dma_start(w1_raw[:].bitcast(I32), w1_words[0].bitcast(I32))
        dw_win = keep.tile([P, TABLE], U32, name="dw_win", tag="dw_win_then_z", align_bytes=64)
        nc.sync.dma_start(dw_win[:].bitcast(I32), d_words[0].rearrange("p n t -> p (n t)").bitcast(I32))
        gs_t = sb("gs_t", [P, PACK], F32)
        nc.sync.dma_start(gs_t[:], gs.rearrange("(p t) o -> p (t o)", t=PACK))
        n1_t = load_list("n1_t", n1, PAIRS // 16)
        n2_t = load_list("n2_t", n2, PAIRS // 16)
        n3_t = load_list("n3_t", n3, S // 16)

        def place_rows(plane, src, rows):
            for r in rows:
                nc.sync.dma_start(plane[:].bitcast(I32)[r:P:32, :], src[:].bitcast(I32)[8 * r : P : 32, :])

        w1_deal = sb("w1_deal", [P, 2 * H], U8)
        nc.scalar.copy(
            w1_deal[:].bitcast(U16).rearrange("p (t m) -> p t m", t=PACK),
            w1_raw[:].bitcast(U16).rearrange("p (m t) -> p t m", t=PACK),
        )

        xs_pick = sb("xs_pick", [P, S], U8)
        nc.vector.tensor_copy(xs_pick[:], xs_win[:].indirect(offs_t[:]))
        nc.vector.tensor_copy(xs_plane[:].bitcast(I32), xs_pick[:].bitcast(I32))
        place_rows(xs_plane, xs_pick, range(1, 4))

        ds_pick = keep.tile([P, H], U8, name="ds_pick", tag="dw_then_z", align_bytes=64)
        nc.vector.tensor_copy(ds_pick[:], ds_win[:].indirect(k1_t[:]))
        ds_deal = sb("ds_deal", [P, H], U8)
        nc.vector.tensor_copy(
            ds_deal[:].rearrange("p (t m) -> p t m", t=PACK), ds_pick[:].rearrange("p (m t) -> p t m", t=PACK)
        )
        place_rows(ds_plane, ds_deal, range(4))

        w1s_deal = sb("w1s_deal", [P, H], U8)
        nc.vector.tensor_copy(
            w1s_deal[:].rearrange("p (t m) -> p t m", t=PACK), w1s_raw[:].rearrange("p (m t) -> p t m", t=PACK)
        )

        xw_pick = [sb("xw_pick%d" % c, [P, HALF], U32) for c in range(2)]
        for c in range(2):
            nc.vector.tensor_copy(xw_pick[c][:], xw_win[:].indirect(offs_t[:, 16 * c : 16 * c + 16]))

        def first_product(out_ap, t, lo, width):
            c = lo // HALF
            nc.tensor.matmul_mx(
                out=out_ap,
                lhsT=w1_deal[:, 2 * P * t : 2 * P * (t + 1)].bitcast(FP4X4),
                lhsT_scale=w1s_deal[:, P * t : P * (t + 1)],
                rhs=xw_pick[c][:, lo - c * HALF : lo - c * HALF + width].bitcast(FP8X4),
                rhs_scale=xs_plane[:, lo : lo + width],
                start=True,
                stop=True,
            )

        z_planes = sb("z_planes", [P, PACK, HALF], BF16)
        for u in range(2):
            y_bank = psum.tile([P, 2, HALF], F32, name="y_bank0%d" % u)
            for a in range(2):
                first_product(y_bank[:, a, :], 2 * u + a, 0, HALF)
            for a in range(2):
                t = 2 * u + a
                nc.scalar.activation(z_planes[:, t, :], y_bank[:, a, :], COPY, scale=gs_t[:, t : t + 1])
        y_quads = [psum.tile([P, PACK, P], F32, name="y_bank1%d" % u) for u in range(2)]
        for u in range(2):
            for t in range(PACK):
                first_product(y_quads[u][:, t, :], t, HALF + u * P, P)

        dw_pick = keep.tile([P, H], U32, name="dw_pick", tag="dw_then_z", align_bytes=64)
        nc.vector.tensor_copy(dw_pick[:], dw_win[:].indirect(k1_t[:]))
        dw_deal = sb("dw_deal", [P, PACK, P], U32)
        dw_by_tile = dw_pick[:].rearrange("p (m t) -> p t m", t=PACK)
        nc.vector.tensor_copy(dw_deal[:, 0, :], dw_by_tile[:, 0, :])

        z_rows = [
            sb("z_rows0", [P, HALF, PACK], BF16),
            keep.tile([P, HALF, PACK], BF16, name="z_rows1", tag="dw_win_then_z", align_bytes=64),
        ]
        z_codes = sb("z_codes", [P, S], U32)
        z_scales = sb("z_scales", [P, S], U8)

        def quantise(c):
            nc.vector.quantize_mx(
                out=z_codes[:, c * HALF : (c + 1) * HALF].bitcast(FP8X4),
                scales=z_scales[:, c * HALF : (c + 1) * HALF],
                in_=z_rows[c][:].rearrange("p n t -> p (n t)"),
            )

        for u in range(2):
            nc.vector.tensor_tensor(
                z_rows[1][:, u * P : (u + 1) * P, :],
                y_quads[u][:].rearrange("p t n -> p n t"),
                gs_t[:].unsqueeze(1).to_broadcast([P, P, PACK]),
                MULT,
            )
        nc.scalar.copy(
            z_rows[0][:, :P, :].rearrange("p (c i) t -> p c t i", i=4),
            z_planes[:, :, :P].rearrange("p t (c i) -> p c t i", i=4),
        )
        nc.vector.tensor_copy(
            z_rows[0][:, P:, :].rearrange("p (c i) t -> p c t i", i=4),
            z_planes[:, :, P:].rearrange("p t (c i) -> p c t i", i=4),
        )
        quantise(1)
        quantise(0)
        nc.vector.tensor_copy(dw_deal[:, 1:, :], dw_by_tile[:, 1:, :])

        h_first = psum.tile([P, 2, HALF], F32, name="h_first", tag="y_bank10")
        h_banks = {}

        def second_product(out_ap, t, cols):
            nc.tensor.matmul_mx(
                out=out_ap,
                lhsT=dw_deal[:, t, :].bitcast(FP8X4),
                lhsT_scale=ds_plane[:, P * t : P * (t + 1)],
                rhs=z_codes[:, cols].bitcast(FP8X4),
                rhs_scale=z_scales[:, cols],
                start=True,
                stop=True,
            )

        def whole_product(t):
            h_banks[t] = psum.tile([P, S], F32, name="h_bank%d" % t, tag="h_bank%d" % (t % 2))
            second_product(h_banks[t][:], t, slice(0, S))

        h_banks[0] = psum.tile([P, S], F32, name="h_bank0", tag="h_bank0")
        second_product(h_first[:, 0, :], 0, slice(HALF, S))
        second_product(h_banks[0][:, :HALF], 0, slice(0, HALF))
        whole_product(1)

        out_rows = out.rearrange("(p t) j -> p t j", t=PACK)
        dt = [sb("dt%d" % t, [P, S], F32) for t in range(PACK)]
        h = {}
        pa = [sb("pa%d" % t, [P, PAIRS], F32) for t in range(PACK)]
        nb = [sb("nb%d" % t, [P, PAIRS], F32) for t in range(PACK)]
        pb = [
            keep.tile([P, PAIRS], F32, name="pb%d" % t, tag="pb_then_res%d" % t, align_bytes=64) for t in range(PACK)
        ]
        other = {}

        def new_h(t):
            h[t] = keep.tile([P, S], F32, name="h%d" % t, tag="h_then_other%d" % max(t, 1), align_bytes=64)

        def leave_psum(t):
            new_h(t)
            nc.scalar.activation(h[t][:], h_banks[t][:], COPY, scale=0.0625)

        def fetch_pairs(t):
            if t == 0:
                nc.vector.tensor_copy(pa[t][:], h[t][:].indirect(n1_t[:]))
            else:
                nc.scalar.activation(pa[t][:], h[t][:].indirect(n1_t[:]), COPY)
            nc.scalar.activation(pb[t][:], h[t][:].indirect(n2_t[:]), COPY)
            nc.scalar.activation(nb[t][:], pb[t][:], COPY, scale=-1.0)

        def put_sums(t):
            nc.vector.tensor_tensor(dt[t][:].indirect(n1_t[:]), pa[t][:], pb[t][:], ADD)

        def put_differences(t):
            nc.vector.tensor_tensor(dt[t][:].indirect(n2_t[:]), pa[t][:], nb[t][:], ADD)

        def fetch_other(t, widths):
            other[t] = keep.tile([P, S], F32, name="other%d" % t, tag="h_then_other%d" % (t + 1), align_bytes=64)
            lo = 0
            for w in widths:
                nc.scalar.activation(
                    other[t][:, lo : lo + w], dt[t][:].indirect(n3_t[:, lo // 16 : (lo + w) // 16]), COPY
                )
                lo = lo + w

        def finish(t, widths):
            res = keep.tile([P, S], F32, name="res%d" % t, tag="pb_then_res%d" % (t + 2), align_bytes=64)
            lo = 0
            for w in widths:
                cols = slice(lo, lo + w)
                nc.vector.tensor_tensor(res[:, cols], dt[t][:, cols], other[t][:, cols], MAX)
                nc.sync.dma_start(out_rows[:, t, cols], res[:, cols])
                lo = lo + w

        new_h(0)
        nc.scalar.activation(h[0][:, HALF:], h_first[:, 0, :], COPY, scale=0.0625)
        nc.scalar.activation(h[0][:, :HALF], h_banks[0][:, :HALF], COPY, scale=0.0625)
        fetch_pairs(0)
        put_sums(0)
        put_differences(0)
        leave_psum(1)
        fetch_pairs(1)
        put_sums(1)
        put_differences(1)
        for t in range(2, PACK):
            whole_product(t)
            leave_psum(t)
        for t in range(2, PACK):
            fetch_other(t - 2, [256, 256])
            fetch_pairs(t)
            put_sums(t)
            finish(t - 2, [512])
            put_differences(t)
        fetch_other(2, [256, 256])
        finish(2, [512])
        fetch_other(3, [256, 128, 128])
        finish(3, [256, 128, 128])
